import numpy as np
import ml_dtypes


def mxq(x, axis, fmt="e4m3"):
    dtype, down = {"e4m3": (ml_dtypes.float8_e4m3fn, 7), "e5m2": (ml_dtypes.float8_e5m2, 14)}[fmt]
    v = np.moveaxis(np.asarray(x, np.float32).astype(ml_dtypes.bfloat16).astype(np.float64), axis, -1)
    blocks = v.reshape(v.shape[:-1] + (-1, 32))
    amax = np.abs(blocks).max(-1, keepdims=True)
    byte = np.maximum(np.where(amax > 0, np.frexp(amax)[1] - 1 + 127, 0) - down, 1)
    scale = np.exp2(byte - 127.0)
    codes = (blocks / scale).astype(np.float32).astype(dtype).astype(np.float64)
    return np.moveaxis((codes * scale).reshape(v.shape), -1, axis)


WIDE = False


def mx_kscale(k):
    if not WIDE:
        return np.ones(k)
    levels = np.array([10, -10, 5, -5, 0])
    if k % 512:
        return np.exp2(np.random.permutation(np.resize(levels, k // 32))).repeat(32)
    a = np.empty((k // 512, 16))
    for p in range(k // 512):
        a[p, :8] = np.random.permutation(np.resize(levels, 8))
        for g in range(8):
            far = levels[np.abs(levels - a[p, g]) >= 10]
            a[p, g + 8] = far[np.random.randint(len(far))]
    return np.exp2(a.ravel()).repeat(32)


def f64(x):
    return np.asarray(x).astype(np.float64)


def striped(idx):
    return np.tile(idx.reshape(-1, 16).T, (8, 1)).astype(np.uint16)


def unstriped(offs):
    return offs[:16].T.reshape(-1).astype(np.int64)


E2M1 = np.array([0.0, 0.5, 1.0, 1.5, 2.0, 3.0, 4.0, 6.0, -0.0, -0.5, -1.0, -1.5, -2.0, -3.0, -4.0, -6.0])


def pack_weight(w, fmt):
    k, n = w.shape
    w = f64(np.asarray(w, np.float32).astype(ml_dtypes.bfloat16)).reshape(k // 32, 32, n)
    amax = np.abs(w).max(1)
    if fmt == "e4m3":
        byte = np.frexp(amax)[1] - 1 + 127 - 7
    else:
        mant, ex = np.frexp(amax / 6.0)
        byte = np.where(mant > 0.5, ex, ex - 1) + 127
    byte = np.clip(np.where(amax > 0, byte, 1), 1, 254)
    scaled = (w * np.exp2(127.0 - byte)[:, None, :]).reshape(k, n).astype(np.float32)
    by_word = np.ascontiguousarray(scaled.reshape(k // 512, 128, 4, n).transpose(0, 1, 3, 2))
    if fmt == "e4m3":
        words = by_word.astype(ml_dtypes.float8_e4m3fn).view(np.uint8)
    else:
        c = by_word.astype(ml_dtypes.float4_e2m1fn).view(np.uint8) & 0xF
        words = (c[..., 0::2] | (c[..., 1::2] << 4)).reshape(k // 512, 128, 2 * n)
    return np.ascontiguousarray(words), np.ascontiguousarray(byte.astype(np.uint8).reshape(k // 512, 16, n))


def unpack_weight(words, scales, fmt):
    g, _, n = scales.shape
    words = np.ascontiguousarray(words).reshape(g, 128, n, -1)
    if fmt == "e4m3":
        vals = words.view(ml_dtypes.float8_e4m3fn).astype(np.float64)
    else:
        nib = np.empty((g, 128, n, 4), np.uint8)
        nib[..., 0::2] = words & 0xF
        nib[..., 1::2] = words >> 4
        vals = E2M1[nib]
    vals = vals * np.repeat(np.exp2(scales.astype(np.float64) - 127.0), 8, axis=1)[..., None]
    return vals.transpose(0, 1, 3, 2).reshape(g * 512, n)


def silu(v):
    return v / (1.0 + np.exp(-np.maximum(v, -700.0)))


K, T, S1, S2 = 512, 1024, 512, 512


def setup_inputs():
    n = np.random.standard_normal
    s = mx_kscale(K)
    u = mx_kscale(K)
    first, second = np.random.permutation(T)[:S1], np.random.permutation(T)[:S2]
    xf = n((K, T))
    x = pack_weight(xf * s[:, None], "e4m3")
    w1 = pack_weight(n((K, K)) / np.sqrt(K) / s[:, None] * u, "e2m1")
    w2 = pack_weight(n((K, K)) / np.sqrt(K) / u[:, None] * u, "e2m1")
    return {
        "x_words": x[0],
        "x_scales": x[1],
        "xr": (xf * u[:, None]).astype(np.float32),
        "w1_words": w1[0],
        "w1_scales": w1[1],
        "w2_words": w2[0],
        "w2_scales": w2[1],
        "gate1": (np.tile(np.random.uniform(0.2, 1.0, S1), (128, 1))).astype(np.float32),
        "gate2": (np.tile(np.random.uniform(0.2, 1.0, S2), (128, 1))).astype(np.float32),
        "offs": striped(first),
        "offs2": striped(second),
    }


def reference(x_words, x_scales, xr, w1_words, w1_scales, w2_words, w2_scales, gate1, gate2, offs, offs2):
    w1 = unpack_weight(w1_words, w1_scales, "e2m1")
    w2 = unpack_weight(w2_words, w2_scales, "e2m1")
    idx, idx2 = unstriped(offs), unstriped(offs2)
    r = f64(xr)
    r[:, idx] += f64(gate1[:1]) * silu(w1.T @ unpack_weight(x_words, x_scales, "e4m3")[:, idx])
    r2 = r.copy()
    r2[:, idx2] += f64(gate2[:1]) * silu(w2.T @ mxq(r[:, idx2], 0, "e4m3"))
    return r2

@@ -1,0 +1,175 @@
+from contextlib import ExitStack
+
+import concourse.mybir as mybir
+
+K, T, S = 512, 1024, 512
+FLOPS = 2 * 2 * K * K * S
+
+F32 = mybir.dt.float32
+BF16 = mybir.dt.bfloat16
+I32 = mybir.dt.int32
+U32 = mybir.dt.uint32
+U16 = mybir.dt.uint16
+U8 = mybir.dt.uint8
+FP8X4 = mybir.dt.float8_e4m3fn_x4
+FP4X4 = mybir.dt.float4_e2m1fn_x4
+MULT = mybir.AluOpType.mult
+ADD = mybir.AluOpType.add
+SILU = mybir.ActivationFunctionType.Silu
+COPY = mybir.ActivationFunctionType.Copy
+
+P = 128
+PACK = 4
+LAST = PACK - 1
+HEAD = slice(0, 128)
+REST = slice(128, S)
+WHOLE = slice(0, S)
+PIECES = [(0, HEAD), (1, HEAD), (0, REST), (1, REST), (2, WHOLE), (3, WHOLE)]
+
+
+def entries(offsets, slots):
+    return offsets[:, slots.start // 16 : slots.stop // 16]
+
+
+def passes(slots):
+    if slots == REST:
+        return [slice(128, 256), slice(256, 512)]
+    return [slots]
+
+
+def load_scale_rows(nc, plane, rows):
+    for q in range(4):
+        nc.sync.dma_start(out=plane[32 * q : 32 * q + 4, :].bitcast(I32), in_=rows[0, 4 * q : 4 * q + 4, :].bitcast(I32))
+
+
+def permute_columns(nc, dst, src):
+    nc.vector.tensor_copy(out=dst.rearrange("p (t m) -> p t m", t=PACK), in_=src.rearrange("p (m t) -> p t m", t=PACK))
+
+
+def tile_moe_mod_silu_kernel(
+    tc, x_words, x_scales, xr, w1_words, w1_scales, w2_words, w2_scales, gate1, gate2, offs, offs2, out
+):
+    nc = tc.nc
+    xr_rows = xr.rearrange("(p t) n -> t p n", t=PACK)
+    out_rows = out.rearrange("(p t) n -> t p n", t=PACK)
+
+    with ExitStack() as ctx:
+        keep = ctx.enter_context(tc.tile_pool(name="keep", bufs=1))
+        psum = ctx.enter_context(tc.psum_pool(name="psum", bufs=1))
+
+        def tile(shape, dtype, name):
+            return keep.tile(shape, dtype, name=name, align_bytes=64)
+
+        list1 = tile([P, S // 16], U16, "list1")
+        list2 = tile([P, S // 16], U16, "list2")
+        xw = tile([P, T], I32, "xw")
+        xs = tile([P, T], U8, "xs")
+        w1_raw = tile([P, 2 * K], U8, "w1_raw")
+        w2_raw = tile([P, 2 * K], U8, "w2_raw")
+        s1_raw = tile([P, K], U8, "s1_raw")
+        s2_raw = tile([P, K], U8, "s2_raw")
+        w1 = tile([P, 2 * K], U8, "w1")
+        w2 = tile([P, 2 * K], U8, "w2")
+        s1 = tile([P, K], U8, "s1")
+        s2 = tile([P, K], U8, "s2")
+        g1 = tile([P, S], F32, "g1")
+        g2 = tile([P, S], F32, "g2")
+        res = [tile([P, T], F32, "res%d" % t) for t in range(PACK)]
+        r = [tile([P, T], F32, "r%d" % t) for t in range(PACK)]
+        r_bf = [tile([P, T], BF16, "r_bf%d" % t) for t in range(LAST)]
+        o = [tile([P, T], F32, "o%d" % t) for t in range(LAST)]
+        win1 = [tile([P, T], F32, "win1_%d" % b) for b in range(3)]
+        win2 = [tile([P, T], F32, "win2_%d" % b) for b in range(2)]
+        xw_g = tile([P, S], I32, "xw_g")
+        xs_g = tile([P, S], U8, "xs_g")
+        y = [tile([P, S], F32, "y%d" % t) for t in range(PACK)]
+        yg = [tile([P, S], F32, "yg%d" % t) for t in range(PACK)]
+        z = [tile([P, S], F32, "z%d" % t) for t in range(PACK)]
+        zg = [tile([P, S], F32, "zg%d" % t) for t in range(PACK)]
+        r_last_g = tile([P, S], F32, "r_last_g")
+        o_last_g = tile([P, S], F32, "o_last_g")
+        grouped = tile([P, S, PACK], BF16, "grouped")
+        r_codes = tile([P, S], U32, "r_codes")
+        r_scales = tile([P, S], U8, "r_scales")
+
+        for plane in (s1_raw, xs, s2_raw):
+            nc.vector.memset(plane[:].bitcast(I32), 0)
+
+        nc.sync.dma_start(out=w1_raw[:].bitcast(I32), in_=w1_words[0].bitcast(I32))
+        load_scale_rows(nc, s1_raw, w1_scales)
+        nc.sync.dma_start(out=xw[:], in_=x_words[0].rearrange("p n t -> p (n t)").bitcast(I32))
+        nc.sync.dma_start(list1[:], offs)
+        load_scale_rows(nc, xs, x_scales)
+        nc.sync.dma_start(out=g1[:], in_=gate1)
+        nc.sync.dma_start(out=res[0][:], in_=xr_rows[0])
+        nc.sync.dma_start(out=res[1][:], in_=xr_rows[1])
+        nc.sync.dma_start(list2[:], offs2)
+        load_scale_rows(nc, s2_raw, w2_scales)
+        nc.sync.dma_start(out=w2_raw[:].bitcast(I32), in_=w2_words[0].bitcast(I32))
+        nc.sync.dma_start(out=res[2][:], in_=xr_rows[2])
+        nc.sync.dma_start(out=res[3][:], in_=xr_rows[3])
+        nc.sync.dma_start(out=g2[:], in_=gate2)
+
+        for w in win1:
+            nc.vector.memset(w[:], 0.0)
+        for w in win2:
+            nc.scalar.activation(w[:], win1[2][:], SILU)
+
+        permute_columns(nc, w1[:].bitcast(U16), w1_raw[:].bitcast(U16))
+        permute_columns(nc, s1[:], s1_raw[:])
+
+        nc.vector.tensor_copy(xw_g[:].bitcast(U32), xw[:].bitcast(U32).indirect(list1[:]))
+        for slots in (HEAD, REST):
+            nc.vector.tensor_copy(xs_g[:, slots], xs[:].indirect(entries(list1, slots)))
+
+        def products(words, scales, codes, code_scales, act, gated, gate):
+            for n, (t, slots) in enumerate(PIECES):
+                acc = psum.tile([P, S], F32, name="acc%d" % n)
+                for cols in passes(slots):
+                    nc.tensor.matmul_mx(
+                        out=acc[:, cols],
+                        lhsT=words[:, 2 * P * t : 2 * P * (t + 1)].bitcast(FP4X4),
+                        lhsT_scale=scales[:, P * t : P * (t + 1)],
+                        rhs=codes[:, cols].bitcast(FP8X4),
+                        rhs_scale=code_scales[:, cols],
+                        start=True,
+                        stop=True,
+                    )
+                nc.scalar.activation(act[t][:, slots], acc[:, slots], SILU)
+                nc.gpsimd.tensor_tensor(gated[t][:, slots], act[t][:, slots], gate[:, slots], MULT)
+
+        products(w1, s1, xw_g, xs_g, y, yg, g1)
+
+        for t, slots in PIECES:
+            window = win1[t % 3]
+            nc.vector.tensor_copy(window[:].indirect(entries(list1, slots)), yg[t][:, slots])
+            if slots.stop == S and t != LAST:
+                nc.gpsimd.tensor_tensor(r[t][:], res[t][:], window[:], ADD)
+                nc.scalar.copy(r_bf[t][:], r[t][:])
+                nc.scalar.activation(grouped[:, :, t], r_bf[t][:].indirect(list2[:]), COPY)
+        nc.vector.tensor_tensor(r[LAST][:], res[LAST][:], win1[LAST % 3][:], ADD)
+        for slots in (HEAD, REST):
+            nc.vector.tensor_copy(r_last_g[:, slots], r[LAST][:].indirect(entries(list2, slots)))
+        permute_columns(nc, w2[:].bitcast(U16), w2_raw[:].bitcast(U16))
+        permute_columns(nc, s2[:], s2_raw[:])
+        for cols in [HEAD] + passes(REST):
+            nc.scalar.copy(grouped[:, cols, LAST], r_last_g[:, cols])
+            nc.vector.quantize_mx(
+                out=r_codes[:, cols].bitcast(FP8X4),
+                scales=r_scales[:, cols],
+                in_=grouped[:, cols, :].rearrange("p s t -> p (s t)"),
+            )
+
+        products(w2, s2, r_codes, r_scales, z, zg, g2)
+        nc.gpsimd.tensor_tensor(o_last_g[:], zg[LAST][:], r_last_g[:], ADD)
+
+        for t, slots in PIECES:
+            if t == LAST:
+                nc.vector.tensor_copy(r[t][:].indirect(entries(list2, slots)), o_last_g[:, slots])
+                nc.sync.dma_start(out=out_rows[t], in_=r[t][:])
+            else:
+                window = win2[t % 2]
+                nc.vector.tensor_copy(window[:].indirect(entries(list2, slots)), zg[t][:, slots])
+                if slots.stop == S:
+                    nc.gpsimd.tensor_tensor(o[t][:], r[t][:], window[:], ADD)
+                    nc.sync.dma_start(out=out_rows[t], in_=o[t][:])

@@ -122,7 +122,7 @@ def tile_moe_mod_silu_kernel(
         for slots in (HEAD, REST):
             nc.vector.tensor_copy(xs_g[:, slots], xs[:].indirect(entries(list1, slots)))
 
-        def products(words, scales, codes, code_scales, act, gated, gate):
+        def products(words, scales, codes, code_scales, act):
             for n, (t, slots) in enumerate(PIECES):
                 acc = psum.tile([P, S], F32, name="acc%d" % n)
                 for cols in passes(slots):
@@ -136,22 +136,41 @@ def tile_moe_mod_silu_kernel(
                         stop=True,
                     )
                 nc.scalar.activation(act[t][:, slots], acc[:, slots], SILU)
-                nc.gpsimd.tensor_tensor(gated[t][:, slots], act[t][:, slots], gate[:, slots], MULT)
 
-        products(w1, s1, xw_g, xs_g, y, yg, g1)
+        def gate(gated, act, g, t, slots):
+            nc.vector.tensor_tensor(gated[t][:, slots], act[t][:, slots], g[:, slots], MULT)
 
-        for t, slots in PIECES:
-            window = win1[t % 3]
-            nc.vector.tensor_copy(window[:].indirect(entries(list1, slots)), yg[t][:, slots])
-            if slots.stop == S and t != LAST:
-                nc.gpsimd.tensor_tensor(r[t][:], res[t][:], window[:], ADD)
+        def scatter(window, offsets, values, slots):
+            nc.vector.tensor_copy(window[:].indirect(entries(offsets, slots)), values[:, slots])
+
+        def make_r(t):
+            nc.vector.tensor_tensor(r[t][:], res[t][:], win1[t % 3][:], ADD)
+            if t != LAST:
                 nc.scalar.copy(r_bf[t][:], r[t][:])
                 nc.scalar.activation(grouped[:, :, t], r_bf[t][:].indirect(list2[:]), COPY)
-        nc.vector.tensor_tensor(r[LAST][:], res[LAST][:], win1[LAST % 3][:], ADD)
+
+        def make_out(t, cols):
+            nc.vector.tensor_tensor(o[t][:, cols], r[t][:, cols], win2[t % 2][:, cols], ADD)
+            nc.sync.dma_start(out=out_rows[t][:, cols], in_=o[t][:, cols])
+
+        products(w1, s1, xw_g, xs_g, y)
+        for slots in (HEAD, REST):
+            for t in (0, 1):
+                gate(yg, y, g1, t, slots)
+            for t in (0, 1):
+                scatter(win1[t], list1, yg[t], slots)
+        make_r(0)
+        gate(yg, y, g1, 2, WHOLE)
+        make_r(1)
+        scatter(win1[2], list1, yg[2], WHOLE)
+        gate(yg, y, g1, 3, WHOLE)
+        make_r(2)
+        scatter(win1[0], list1, yg[3], WHOLE)
+        permute_columns(nc, w2[:].bitcast(U16), w2_raw[:].bitcast(U16))
+        make_r(3)
+        permute_columns(nc, s2[:], s2_raw[:])
         for slots in (HEAD, REST):
             nc.vector.tensor_copy(r_last_g[:, slots], r[LAST][:].indirect(entries(list2, slots)))
-        permute_columns(nc, w2[:].bitcast(U16), w2_raw[:].bitcast(U16))
-        permute_columns(nc, s2[:], s2_raw[:])
         for cols in [HEAD] + passes(REST):
             nc.scalar.copy(grouped[:, cols, LAST], r_last_g[:, cols])
             nc.vector.quantize_mx(
@@ -160,16 +179,19 @@ def tile_moe_mod_silu_kernel(
                 in_=grouped[:, cols, :].rearrange("p s t -> p (s t)"),
             )
 
-        products(w2, s2, r_codes, r_scales, z, zg, g2)
-        nc.gpsimd.tensor_tensor(o_last_g[:], zg[LAST][:], r_last_g[:], ADD)
-
-        for t, slots in PIECES:
-            if t == LAST:
-                nc.vector.tensor_copy(r[t][:].indirect(entries(list2, slots)), o_last_g[:, slots])
-                nc.sync.dma_start(out=out_rows[t], in_=r[t][:])
-            else:
-                window = win2[t % 2]
-                nc.vector.tensor_copy(window[:].indirect(entries(list2, slots)), zg[t][:, slots])
-                if slots.stop == S:
-                    nc.gpsimd.tensor_tensor(o[t][:], r[t][:], window[:], ADD)
-                    nc.sync.dma_start(out=out_rows[t], in_=o[t][:])
+        products(w2, s2, r_codes, r_scales, z)
+        for slots in (HEAD, REST):
+            for t in (0, 1):
+                gate(zg, z, g2, t, slots)
+            for t in (0, 1):
+                scatter(win2[t], list2, zg[t], slots)
+        make_out(0, slice(0, T))
+        gate(zg, z, g2, LAST, WHOLE)
+        make_out(1, slice(0, T))
+        nc.vector.tensor_tensor(o_last_g[:], zg[LAST][:], r_last_g[:], ADD)
+        gate(zg, z, g2, 2, WHOLE)
+        scatter(r[LAST], list2, o_last_g, WHOLE)
+        nc.sync.dma_start(out=out_rows[LAST], in_=r[LAST][:])
+        scatter(win2[0], list2, zg[2], WHOLE)
+        for cols in (slice(0, 512), slice(512, 768), slice(768, T)):
+            make_out(2, cols)

@@ -1,6 +1,7 @@
 from contextlib import ExitStack
 
 import concourse.mybir as mybir
+from concourse.masks import make_identity
 
 K, T, S = 512, 1024, 512
 FLOPS = 2 * 2 * K * K * S
@@ -21,24 +22,21 @@ COPY = mybir.ActivationFunctionType.Copy
 P = 128
 PACK = 4
 LAST = PACK - 1
-HEAD = slice(0, 128)
-REST = slice(128, S)
+BANK = 512
+A = slice(0, 128)
+B = slice(128, 256)
+C = slice(256, S)
+BC = slice(128, S)
 WHOLE = slice(0, S)
-PIECES = [(0, HEAD), (1, HEAD), (0, REST), (1, REST), (2, WHOLE), (3, WHOLE)]
+HALVES = (slice(0, BANK), slice(BANK, T))
 
 
 def entries(offsets, slots):
     return offsets[:, slots.start // 16 : slots.stop // 16]
 
 
-def passes(slots):
-    if slots == REST:
-        return [slice(128, 256), slice(256, 512)]
-    return [slots]
-
-
-def load_scale_rows(nc, plane, rows):
-    for q in range(4):
+def load_scale_rows(nc, plane, rows, quadrants):
+    for q in quadrants:
         nc.sync.dma_start(out=plane[32 * q : 32 * q + 4, :].bitcast(I32), in_=rows[0, 4 * q : 4 * q + 4, :].bitcast(I32))
 
 
@@ -57,8 +55,11 @@ def tile_moe_mod_silu_kernel(
         keep = ctx.enter_context(tc.tile_pool(name="keep", bufs=1))
         psum = ctx.enter_context(tc.psum_pool(name="psum", bufs=1))
 
-        def tile(shape, dtype, name):
-            return keep.tile(shape, dtype, name=name, align_bytes=64)
+        def tile(shape, dtype, name, after=None):
+            return keep.tile(shape, dtype, name=name, tag=after or name, align_bytes=64)
+
+        def bank(n):
+            return psum.tile([P, BANK], F32, name="bank%d" % n)
 
         list1 = tile([P, S // 16], U16, "list1")
         list2 = tile([P, S // 16], U16, "list2")
@@ -69,129 +70,229 @@ def tile_moe_mod_silu_kernel(
         s1_raw = tile([P, K], U8, "s1_raw")
         s2_raw = tile([P, K], U8, "s2_raw")
         w1 = tile([P, 2 * K], U8, "w1")
-        w2 = tile([P, 2 * K], U8, "w2")
         s1 = tile([P, K], U8, "s1")
-        s2 = tile([P, K], U8, "s2")
         g1 = tile([P, S], F32, "g1")
         g2 = tile([P, S], F32, "g2")
         res = [tile([P, T], F32, "res%d" % t) for t in range(PACK)]
-        r = [tile([P, T], F32, "r%d" % t) for t in range(PACK)]
-        r_bf = [tile([P, T], BF16, "r_bf%d" % t) for t in range(LAST)]
-        o = [tile([P, T], F32, "o%d" % t) for t in range(LAST)]
-        win1 = [tile([P, T], F32, "win1_%d" % b) for b in range(3)]
-        win2 = [tile([P, T], F32, "win2_%d" % b) for b in range(2)]
+        win1 = [tile([P, T], F32, "win1_%d" % b) for b in range(2)]
         xw_g = tile([P, S], I32, "xw_g")
         xs_g = tile([P, S], U8, "xs_g")
         y = [tile([P, S], F32, "y%d" % t) for t in range(PACK)]
-        yg = [tile([P, S], F32, "yg%d" % t) for t in range(PACK)]
         z = [tile([P, S], F32, "z%d" % t) for t in range(PACK)]
-        zg = [tile([P, S], F32, "zg%d" % t) for t in range(PACK)]
-        r_last_g = tile([P, S], F32, "r_last_g")
-        o_last_g = tile([P, S], F32, "o_last_g")
-        grouped = tile([P, S, PACK], BF16, "grouped")
+        grouped_a = tile([P, P, PACK], BF16, "grouped_a")
+        grouped_bc = tile([P, S - P, PACK], BF16, "grouped_bc")
         r_codes = tile([P, S], U32, "r_codes")
         r_scales = tile([P, S], U8, "r_scales")
+        zero = tile([P, 1], F32, "zero")
 
         for plane in (s1_raw, xs, s2_raw):
             nc.vector.memset(plane[:].bitcast(I32), 0)
 
-        nc.sync.dma_start(out=w1_raw[:].bitcast(I32), in_=w1_words[0].bitcast(I32))
-        load_scale_rows(nc, s1_raw, w1_scales)
-        nc.sync.dma_start(out=xw[:], in_=x_words[0].rearrange("p n t -> p (n t)").bitcast(I32))
         nc.sync.dma_start(list1[:], offs)
-        load_scale_rows(nc, xs, x_scales)
+        load_scale_rows(nc, s1_raw, w1_scales, (0, 1))
+        nc.scalar.dma_start(out=xw[:], in_=x_words[0].rearrange("p n t -> p (n t)").bitcast(I32))
+        nc.sync.dma_start(out=w1_raw[:].bitcast(I32), in_=w1_words[0].bitcast(I32))
+        load_scale_rows(nc, s1_raw, w1_scales, (2, 3))
+        load_scale_rows(nc, xs, x_scales, range(4))
         nc.sync.dma_start(out=g1[:], in_=gate1)
         nc.sync.dma_start(out=res[0][:], in_=xr_rows[0])
-        nc.sync.dma_start(out=res[1][:], in_=xr_rows[1])
         nc.sync.dma_start(list2[:], offs2)
-        load_scale_rows(nc, s2_raw, w2_scales)
+        nc.sync.dma_start(out=res[1][:], in_=xr_rows[1])
+        load_scale_rows(nc, s2_raw, w2_scales, range(4))
         nc.sync.dma_start(out=w2_raw[:].bitcast(I32), in_=w2_words[0].bitcast(I32))
         nc.sync.dma_start(out=res[2][:], in_=xr_rows[2])
         nc.sync.dma_start(out=res[3][:], in_=xr_rows[3])
         nc.sync.dma_start(out=g2[:], in_=gate2)
 
-        for w in win1:
-            nc.vector.memset(w[:], 0.0)
-        for w in win2:
-            nc.scalar.activation(w[:], win1[2][:], SILU)
+        nc.vector.memset(zero[:], 0.0)
+        nc.vector.memset(win1[0][:], 0.0)
+        nc.scalar.activation(win1[1][:], zero[:].to_broadcast([P, T]), SILU)
 
         permute_columns(nc, w1[:].bitcast(U16), w1_raw[:].bitcast(U16))
         permute_columns(nc, s1[:], s1_raw[:])
+        ident = tile([P, P], F32, "ident", "s1_raw")
+        make_identity(nc, ident[:])
 
         nc.vector.tensor_copy(xw_g[:].bitcast(U32), xw[:].bitcast(U32).indirect(list1[:]))
-        for slots in (HEAD, REST):
+        for slots in (A, BC):
             nc.vector.tensor_copy(xs_g[:, slots], xs[:].indirect(entries(list1, slots)))
+        win1.append(tile([P, T], F32, "win1_2", "xw"))
+        nc.gpsimd.memset(win1[2][:], 0.0)
 
-        def products(words, scales, codes, code_scales, act):
-            for n, (t, slots) in enumerate(PIECES):
-                acc = psum.tile([P, S], F32, name="acc%d" % n)
-                for cols in passes(slots):
-                    nc.tensor.matmul_mx(
-                        out=acc[:, cols],
-                        lhsT=words[:, 2 * P * t : 2 * P * (t + 1)].bitcast(FP4X4),
-                        lhsT_scale=scales[:, P * t : P * (t + 1)],
-                        rhs=codes[:, cols].bitcast(FP8X4),
-                        rhs_scale=code_scales[:, cols],
-                        start=True,
-                        stop=True,
-                    )
-                nc.scalar.activation(act[t][:, slots], acc[:, slots], SILU)
+        def product(n, words, scales, codes, code_scales, act, t, slots):
+            acc = bank(n)
+            for cols in (B, C) if slots == BC else (slots,):
+                nc.tensor.matmul_mx(
+                    out=acc[:, cols],
+                    lhsT=words[:, 2 * P * t : 2 * P * (t + 1)].bitcast(FP4X4),
+                    lhsT_scale=scales[:, P * t : P * (t + 1)],
+                    rhs=codes[:, cols].bitcast(FP8X4),
+                    rhs_scale=code_scales[:, cols],
+                    start=True,
+                    stop=True,
+                )
+            nc.scalar.activation(act[t][:, slots], acc[:, slots], SILU)
 
-        def gate(gated, act, g, t, slots):
-            nc.vector.tensor_tensor(gated[t][:, slots], act[t][:, slots], g[:, slots], MULT)
+        def scatter(window, offsets, act, g, slots):
+            nc.vector.tensor_tensor(window[:].indirect(entries(offsets, slots)), act[:, slots], g[:, slots], MULT)
 
-        def scatter(window, offsets, values, slots):
-            nc.vector.tensor_copy(window[:].indirect(entries(offsets, slots)), values[:, slots])
+        def turn(dst, src, start, stop):
+            for j in range(BANK // P):
+                cols = slice(P * j, P * (j + 1))
+                nc.tensor.matmul(
+                    dst[:, cols], src[:, cols], ident[:],
+                    start=start and j == 0, stop=stop and j == BANK // P - 1, is_transpose=True,
+                )
 
-        def make_r(t):
-            nc.vector.tensor_tensor(r[t][:], res[t][:], win1[t % 3][:], ADD)
-            if t != LAST:
-                nc.scalar.copy(r_bf[t][:], r[t][:])
-                nc.scalar.activation(grouped[:, :, t], r_bf[t][:].indirect(list2[:]), COPY)
+        def plane(t, slots):
+            if slots == A:
+                return grouped_a[:, :, t]
+            return grouped_bc[:, slots.start - P : slots.stop - P, t]
 
-        def make_out(t, cols):
-            nc.vector.tensor_tensor(o[t][:, cols], r[t][:, cols], win2[t % 2][:, cols], ADD)
-            nc.sync.dma_start(out=out_rows[t][:, cols], in_=o[t][:, cols])
+        def gather_r(t, slots):
+            nc.scalar.activation(plane(t, slots), r_bf[t][:].indirect(entries(list2, slots)), COPY)
 
-        products(w1, s1, xw_g, xs_g, y)
-        for slots in (HEAD, REST):
-            for t in (0, 1):
-                gate(yg, y, g1, t, slots)
-            for t in (0, 1):
-                scatter(win1[t], list1, yg[t], slots)
-        make_r(0)
-        gate(yg, y, g1, 2, WHOLE)
-        make_r(1)
-        scatter(win1[2], list1, yg[2], WHOLE)
-        gate(yg, y, g1, 3, WHOLE)
-        make_r(2)
-        scatter(win1[0], list1, yg[3], WHOLE)
+        r_turned, r_bf = {}, {}
+
+        def open_r(t):
+            sums = [bank(2 + 2 * t + h) for h in range(2)]
+            for h in range(2):
+                turn(sums[h], res[t][:, HALVES[h]], True, False)
+            return sums
+
+        def close_r(t, sums):
+            r_turned[t] = tile([P, T], F32, "r_turned%d" % t)
+            r_bf[t] = tile([P, T], BF16, "r_bf%d" % t)
+            for h in range(2):
+                turn(sums[h], win1[t][:, HALVES[h]], False, True)
+                nc.scalar.copy(r_turned[t][:, HALVES[h]], sums[h][:])
+            for h in range(2):
+                back = bank(6 + h)
+                turn(back, r_turned[t][:, HALVES[h]], True, True)
+                nc.scalar.copy(r_bf[t][:, HALVES[h]], back[:])
+
+        pieces1 = [(0, A), (1, A), (0, BC), (1, BC), (2, WHOLE), (3, WHOLE)]
+        for n, (t, slots) in enumerate(pieces1):
+            product(n, w1, s1, xw_g, xs_g, y, t, slots)
+        win2 = [tile([P, T], F32, "win2_%d" % b, after) for b, after in enumerate(("xs", "xw_g", "xs_g"))]
+        for w in win2:
+            nc.gpsimd.memset(w[:], 0.0)
+        sums0 = open_r(0)
+        for t, slots in pieces1[:3]:
+            scatter(win1[t], list1, y[t], g1, slots)
+        close_r(0, sums0)
+        gather_r(0, A)
+        gather_r(0, BC)
+        y_gated = {}
+        for t in (2, 3):
+            y_gated[t] = tile([P, S], F32, "y_gated%d" % t)
+            nc.vector.tensor_tensor(y_gated[t][:], y[t][:], g1[:], MULT)
+        scatter(win1[1], list1, y[1], g1, BC)
+        r_bf[1] = tile([P, T], BF16, "r_bf1", "y3")
+        nc.gpsimd.tensor_tensor(r_bf[1][:], res[1][:], win1[1][:], ADD)
+        gather_r(1, A)
+        gather_r(1, BC)
+        r_turned[1] = tile([P, T], F32, "r_turned1")
+        for h in range(2):
+            sums = bank(3 - h)
+            turn(sums, res[1][:, HALVES[h]], True, False)
+            turn(sums, win1[1][:, HALVES[h]], False, True)
+            nc.scalar.copy(r_turned[1][:, HALVES[h]], sums[:])
+        nc.vector.tensor_copy(win1[2][:].indirect(list1[:]), y_gated[2][:])
+        r_bf[2] = tile([P, T], BF16, "r_bf2")
+        nc.gpsimd.tensor_tensor(r_bf[2][:], res[2][:], win1[2][:], ADD)
+        sums2 = [bank(6 + h) for h in range(2)]
+        for h in range(2):
+            turn(sums2[h], res[2][:, HALVES[h]], True, False)
+        for h in range(2):
+            turn(sums2[h], win1[2][:, HALVES[h]], False, False)
+        nc.vector.tensor_copy(win1[0][:].indirect(list1[:]), y_gated[3][:])
+        w2 = tile([P, 2 * K], U8, "w2", "y_gated2")
+        s2 = tile([P, K], U8, "s2", "y1")
         permute_columns(nc, w2[:].bitcast(U16), w2_raw[:].bitcast(U16))
-        make_r(3)
+        r_bf[LAST] = tile([P, T], BF16, "r_bf3", "res2")
+        nc.vector.tensor_tensor(r_bf[LAST][:], res[LAST][:], win1[0][:], ADD)
         permute_columns(nc, s2[:], s2_raw[:])
-        for slots in (HEAD, REST):
-            nc.vector.tensor_copy(r_last_g[:, slots], r[LAST][:].indirect(entries(list2, slots)))
-        for cols in [HEAD] + passes(REST):
-            nc.scalar.copy(grouped[:, cols, LAST], r_last_g[:, cols])
+        r_end = tile([P, 256], F32, "r_end")
+        nc.vector.tensor_tensor(r_end[:], res[LAST][:, 768:T], win1[0][:, 768:T], ADD)
+
+        def quantize(cols):
+            src = grouped_a[:] if cols == A else grouped_bc[:, cols.start - P : cols.stop - P, :]
             nc.vector.quantize_mx(
                 out=r_codes[:, cols].bitcast(FP8X4),
                 scales=r_scales[:, cols],
-                in_=grouped[:, cols, :].rearrange("p s t -> p (s t)"),
+                in_=src.rearrange("p s t -> p (s t)"),
             )
 
-        products(w2, s2, r_codes, r_scales, z)
-        for slots in (HEAD, REST):
-            for t in (0, 1):
-                gate(zg, z, g2, t, slots)
-            for t in (0, 1):
-                scatter(win2[t], list2, zg[t], slots)
-        make_out(0, slice(0, T))
-        gate(zg, z, g2, LAST, WHOLE)
-        make_out(1, slice(0, T))
-        nc.vector.tensor_tensor(o_last_g[:], zg[LAST][:], r_last_g[:], ADD)
-        gate(zg, z, g2, 2, WHOLE)
-        scatter(r[LAST], list2, o_last_g, WHOLE)
-        nc.sync.dma_start(out=out_rows[LAST], in_=r[LAST][:])
-        scatter(win2[0], list2, zg[2], WHOLE)
-        for cols in (slice(0, 512), slice(512, 768), slice(768, T)):
-            make_out(2, cols)
+        def second(n, t, slots):
+            product(n, w2, s2, r_codes, r_scales, z, t, slots)
+
+        gather_r(2, A)
+        gather_r(3, A)
+        quantize(A)
+        r_begin = tile([P, 768], F32, "r_begin", "grouped_a")
+        nc.vector.tensor_tensor(r_begin[:], res[LAST][:, 0:768], win1[0][:, 0:768], ADD)
+        gather_r(2, B)
+        gather_r(3, B)
+        quantize(B)
+        second(0, 2, A)
+        second(1, 0, A)
+        gather_r(2, C)
+        second(0, 2, B)
+        second(1, 0, B)
+        gather_r(3, C)
+        scatter(win2[0], list2, z[2], g2, A)
+        scatter(win2[1], list2, z[0], g2, A)
+        scatter(win2[0], list2, z[2], g2, B)
+        quantize(C)
+        second(2, 2, C)
+        second(3, 0, C)
+        second(4, 1, WHOLE)
+        second(5, 3, WHOLE)
+
+        def store(t, sums, h, o):
+            nc.scalar.copy(o[:, HALVES[h]], sums[:])
+            nc.sync.dma_start(out=out_rows[t][:, HALVES[h]], in_=o[:, HALVES[h]])
+
+        def open_out(t):
+            sums = [bank(2 + 2 * t + h) for h in range(2)]
+            for h in range(2):
+                turn(sums[h], r_turned[t][:, HALVES[h]], True, False)
+            return sums
+
+        def close_out(t, window, sums, banks):
+            turned = tile([P, T], F32, "turned")
+            o = tile([P, T], F32, "o%d" % t)
+            for h in range(2):
+                fwd = bank(banks[h])
+                turn(fwd, window[:, HALVES[h]], True, True)
+                nc.scalar.copy(turned[:, HALVES[h]], fwd[:])
+            for h in range(2):
+                turn(sums[h], turned[:, HALVES[h]], False, True)
+                store(t, sums[h], h, o)
+
+        def close_forward(t, window, sums, banks):
+            turned = tile([P, T], F32, "turned")
+            o = tile([P, T], F32, "o%d" % t)
+            for h in range(2):
+                turn(sums[h], window[:, HALVES[h]], False, True)
+                nc.scalar.copy(turned[:, HALVES[h]], sums[h][:])
+            for h in range(2):
+                back = bank(banks[h])
+                turn(back, turned[:, HALVES[h]], True, True)
+                store(t, back, h, o)
+
+        sums0 = open_out(0)
+        sums1 = open_out(1)
+        scatter(win2[1], list2, z[0], g2, B)
+        scatter(win2[0], list2, z[2], g2, C)
+        close_forward(2, win2[0], sums2, (0, 1))
+        scatter(win2[1], list2, z[0], g2, C)
+        close_out(0, win2[1], sums0, (7, 6))
+        scatter(win2[2], list2, z[1], g2, WHOLE)
+        close_out(1, win2[2], sums1, (6, 7))
+        scatter(win2[0], list2, z[3], g2, WHOLE)
+        o_last = tile([P, T], F32, "o_last", "turned")
+        for cols, r_part in ((slice(0, 512), r_begin[:, 0:512]), (slice(512, 768), r_begin[:, 512:768]), (slice(768, T), r_end[:])):
+            nc.vector.tensor_tensor(o_last[:, cols], r_part, win2[0][:, cols], ADD)
+            nc.sync.dma_start(out=out_rows[LAST][:, cols], in_=o_last[:, cols])

@@ -74,10 +74,12 @@ def tile_moe_mod_silu_kernel(
         g1 = tile([P, S], F32, "g1")
         g2 = tile([P, S], F32, "g2")
         res = [tile([P, T], F32, "res%d" % t) for t in range(PACK)]
-        win1 = [tile([P, T], F32, "win1_%d" % b) for b in range(2)]
+        win1 = [tile([P, T], F32, "win1_%d" % b) for b in range(3)]
+        win2 = [tile([P, T], F32, "win2_%d" % b) for b in range(2)]
         xw_g = tile([P, S], I32, "xw_g")
         xs_g = tile([P, S], U8, "xs_g")
-        y = [tile([P, S], F32, "y%d" % t) for t in range(PACK)]
+        y_late = tile([P, 2, S], F32, "y_late")
+        y = [tile([P, S], F32, "y%d" % t) for t in range(2)] + [y_late[:, b, :] for b in range(2)]
         z = [tile([P, S], F32, "z%d" % t) for t in range(PACK)]
         grouped_a = tile([P, P, PACK], BF16, "grouped_a")
         grouped_bc = tile([P, S - P, PACK], BF16, "grouped_bc")
@@ -105,8 +107,11 @@ def tile_moe_mod_silu_kernel(
         nc.sync.dma_start(out=g2[:], in_=gate2)
 
         nc.vector.memset(zero[:], 0.0)
-        nc.vector.memset(win1[0][:], 0.0)
-        nc.scalar.activation(win1[1][:], zero[:].to_broadcast([P, T]), SILU)
+        zeros = zero[:].to_broadcast([P, T])
+        for w in win1[:2]:
+            nc.vector.memset(w[:], 0.0)
+        for w in win1[2:] + win2:
+            nc.scalar.activation(w[:], zeros, SILU)
 
         permute_columns(nc, w1[:].bitcast(U16), w1_raw[:].bitcast(U16))
         permute_columns(nc, s1[:], s1_raw[:])
@@ -116,8 +121,6 @@ def tile_moe_mod_silu_kernel(
         nc.vector.tensor_copy(xw_g[:].bitcast(U32), xw[:].bitcast(U32).indirect(list1[:]))
         for slots in (A, BC):
             nc.vector.tensor_copy(xs_g[:, slots], xs[:].indirect(entries(list1, slots)))
-        win1.append(tile([P, T], F32, "win1_2", "xw"))
-        nc.gpsimd.memset(win1[2][:], 0.0)
 
         def product(n, words, scales, codes, code_scales, act, t, slots):
             acc = bank(n)
@@ -174,21 +177,18 @@ def tile_moe_mod_silu_kernel(
         pieces1 = [(0, A), (1, A), (0, BC), (1, BC), (2, WHOLE), (3, WHOLE)]
         for n, (t, slots) in enumerate(pieces1):
             product(n, w1, s1, xw_g, xs_g, y, t, slots)
-        win2 = [tile([P, T], F32, "win2_%d" % b, after) for b, after in enumerate(("xs", "xw_g", "xs_g"))]
-        for w in win2:
-            nc.gpsimd.memset(w[:], 0.0)
+        win2.append(tile([P, T], F32, "win2_2", "xs_g"))
+        nc.scalar.activation(win2[2][:], zeros, SILU)
         sums0 = open_r(0)
         for t, slots in pieces1[:3]:
             scatter(win1[t], list1, y[t], g1, slots)
         close_r(0, sums0)
         gather_r(0, A)
         gather_r(0, BC)
-        y_gated = {}
-        for t in (2, 3):
-            y_gated[t] = tile([P, S], F32, "y_gated%d" % t)
-            nc.vector.tensor_tensor(y_gated[t][:], y[t][:], g1[:], MULT)
         scatter(win1[1], list1, y[1], g1, BC)
-        r_bf[1] = tile([P, T], BF16, "r_bf1", "y3")
+        y_gated = tile([P, 2, S], F32, "y_gated", "win1_0")
+        nc.vector.tensor_tensor(y_gated[:], y_late[:], g1[:].unsqueeze(1).to_broadcast([P, 2, S]), MULT)
+        r_bf[1] = tile([P, T], BF16, "r_bf1", "y_late")
         nc.gpsimd.tensor_tensor(r_bf[1][:], res[1][:], win1[1][:], ADD)
         gather_r(1, A)
         gather_r(1, BC)
@@ -198,7 +198,7 @@ def tile_moe_mod_silu_kernel(
             turn(sums, res[1][:, HALVES[h]], True, False)
             turn(sums, win1[1][:, HALVES[h]], False, True)
             nc.scalar.copy(r_turned[1][:, HALVES[h]], sums[:])
-        nc.vector.tensor_copy(win1[2][:].indirect(list1[:]), y_gated[2][:])
+        nc.vector.tensor_copy(win1[2][:].indirect(list1[:]), y_gated[:, 0, :])
         r_bf[2] = tile([P, T], BF16, "r_bf2")
         nc.gpsimd.tensor_tensor(r_bf[2][:], res[2][:], win1[2][:], ADD)
         sums2 = [bank(6 + h) for h in range(2)]
@@ -206,15 +206,13 @@ def tile_moe_mod_silu_kernel(
             turn(sums2[h], res[2][:, HALVES[h]], True, False)
         for h in range(2):
             turn(sums2[h], win1[2][:, HALVES[h]], False, False)
-        nc.vector.tensor_copy(win1[0][:].indirect(list1[:]), y_gated[3][:])
-        w2 = tile([P, 2 * K], U8, "w2", "y_gated2")
-        s2 = tile([P, K], U8, "s2", "y1")
-        permute_columns(nc, w2[:].bitcast(U16), w2_raw[:].bitcast(U16))
+        nc.vector.tensor_copy(win1[1][:].indirect(list1[:]), y_gated[:, 1, :])
         r_bf[LAST] = tile([P, T], BF16, "r_bf3", "res2")
-        nc.vector.tensor_tensor(r_bf[LAST][:], res[LAST][:], win1[0][:], ADD)
+        nc.vector.tensor_tensor(r_bf[LAST][:], res[LAST][:], win1[1][:], ADD)
+        w2 = tile([P, 2 * K], U8, "w2", "win1_2")
+        permute_columns(nc, w2[:].bitcast(U16), w2_raw[:].bitcast(U16))
+        s2 = tile([P, K], U8, "s2", "w2_raw")
         permute_columns(nc, s2[:], s2_raw[:])
-        r_end = tile([P, 256], F32, "r_end")
-        nc.vector.tensor_tensor(r_end[:], res[LAST][:, 768:T], win1[0][:, 768:T], ADD)
 
         def quantize(cols):
             src = grouped_a[:] if cols == A else grouped_bc[:, cols.start - P : cols.stop - P, :]
@@ -230,8 +228,8 @@ def tile_moe_mod_silu_kernel(
         gather_r(2, A)
         gather_r(3, A)
         quantize(A)
-        r_begin = tile([P, 768], F32, "r_begin", "grouped_a")
-        nc.vector.tensor_tensor(r_begin[:], res[LAST][:, 0:768], win1[0][:, 0:768], ADD)
+        r_last = tile([P, T], F32, "r_last", "grouped_a")
+        nc.vector.tensor_tensor(r_last[:], res[LAST][:], win1[1][:], ADD)
         gather_r(2, B)
         gather_r(3, B)
         quantize(B)
@@ -293,6 +291,6 @@ def tile_moe_mod_silu_kernel(
         close_out(1, win2[2], sums1, (6, 7))
         scatter(win2[0], list2, z[3], g2, WHOLE)
         o_last = tile([P, T], F32, "o_last", "turned")
-        for cols, r_part in ((slice(0, 512), r_begin[:, 0:512]), (slice(512, 768), r_begin[:, 512:768]), (slice(768, T), r_end[:])):
-            nc.vector.tensor_tensor(o_last[:, cols], r_part, win2[0][:, cols], ADD)
+        for cols in (slice(0, 512), slice(512, 768), slice(768, T)):
+            nc.vector.tensor_tensor(o_last[:, cols], r_last[:, cols], win2[0][:, cols], ADD)
             nc.sync.dma_start(out=out_rows[LAST][:, cols], in_=o_last[:, cols])

from contextlib import ExitStack

import concourse.mybir as mybir
from concourse.masks import make_identity

K, T, S = 512, 1024, 512
FLOPS = 2 * 2 * K * K * S

F32 = mybir.dt.float32
BF16 = mybir.dt.bfloat16
I32 = mybir.dt.int32
U32 = mybir.dt.uint32
U16 = mybir.dt.uint16
U8 = mybir.dt.uint8
FP8X4 = mybir.dt.float8_e4m3fn_x4
FP4X4 = mybir.dt.float4_e2m1fn_x4
MULT = mybir.AluOpType.mult
ADD = mybir.AluOpType.add
SILU = mybir.ActivationFunctionType.Silu
COPY = mybir.ActivationFunctionType.Copy

P = 128
PACK = 4
LAST = PACK - 1
BANK = 512
A = slice(0, 128)
B = slice(128, 256)
C = slice(256, S)
BC = slice(128, S)
WHOLE = slice(0, S)
HALVES = (slice(0, BANK), slice(BANK, T))


def entries(offsets, slots):
    return offsets[:, slots.start // 16 : slots.stop // 16]


def load_scale_rows(nc, plane, rows, quadrants):
    for q in quadrants:
        nc.sync.dma_start(out=plane[32 * q : 32 * q + 4, :].bitcast(I32), in_=rows[0, 4 * q : 4 * q + 4, :].bitcast(I32))


def permute_columns(nc, dst, src):
    nc.vector.tensor_copy(out=dst.rearrange("p (t m) -> p t m", t=PACK), in_=src.rearrange("p (m t) -> p t m", t=PACK))


def tile_moe_mod_silu_kernel(
    tc, x_words, x_scales, xr, w1_words, w1_scales, w2_words, w2_scales, gate1, gate2, offs, offs2, out
):
    nc = tc.nc
    xr_rows = xr.rearrange("(p t) n -> t p n", t=PACK)
    out_rows = out.rearrange("(p t) n -> t p n", t=PACK)

    with ExitStack() as ctx:
        keep = ctx.enter_context(tc.tile_pool(name="keep", bufs=1))
        psum = ctx.enter_context(tc.psum_pool(name="psum", bufs=1))

        def tile(shape, dtype, name, after=None):
            return keep.tile(shape, dtype, name=name, tag=after or name, align_bytes=64)

        def bank(n):
            return psum.tile([P, BANK], F32, name="bank%d" % n)

        list1 = tile([P, S // 16], U16, "list1")
        list2 = tile([P, S // 16], U16, "list2")
        xw = tile([P, T], I32, "xw")
        xs = tile([P, T], U8, "xs")
        w1_raw = tile([P, 2 * K], U8, "w1_raw")
        w2_raw = tile([P, 2 * K], U8, "w2_raw")
        s1_raw = tile([P, K], U8, "s1_raw")
        s2_raw = tile([P, K], U8, "s2_raw")
        w1 = tile([P, 2 * K], U8, "w1")
        s1 = tile([P, K], U8, "s1")
        g1 = tile([P, S], F32, "g1")
        g2 = tile([P, S], F32, "g2")
        res = [tile([P, T], F32, "res%d" % t) for t in range(PACK)]
        win1 = [tile([P, T], F32, "win1_%d" % b) for b in range(3)]
        win2 = [tile([P, T], F32, "win2_%d" % b) for b in range(2)]
        xw_g = tile([P, S], I32, "xw_g")
        xs_g = tile([P, S], U8, "xs_g")
        y_late = tile([P, 2, S], F32, "y_late")
        y = [tile([P, S], F32, "y%d" % t) for t in range(2)] + [y_late[:, b, :] for b in range(2)]
        z = [tile([P, S], F32, "z%d" % t) for t in range(PACK)]
        grouped_a = tile([P, P, PACK], BF16, "grouped_a")
        grouped_bc = tile([P, S - P, PACK], BF16, "grouped_bc")
        r_codes = tile([P, S], U32, "r_codes")
        r_scales = tile([P, S], U8, "r_scales")
        zero = tile([P, 1], F32, "zero")

        for plane in (s1_raw, xs, s2_raw):
            nc.vector.memset(plane[:].bitcast(I32), 0)

        nc.sync.dma_start(list1[:], offs)
        load_scale_rows(nc, s1_raw, w1_scales, (0, 1))
        nc.scalar.dma_start(out=xw[:], in_=x_words[0].rearrange("p n t -> p (n t)").bitcast(I32))
        nc.sync.dma_start(out=w1_raw[:].bitcast(I32), in_=w1_words[0].bitcast(I32))
        load_scale_rows(nc, s1_raw, w1_scales, (2, 3))
        load_scale_rows(nc, xs, x_scales, range(4))
        nc.sync.dma_start(out=g1[:], in_=gate1)
        nc.sync.dma_start(out=res[0][:], in_=xr_rows[0])
        nc.sync.dma_start(list2[:], offs2)
        nc.sync.dma_start(out=res[1][:], in_=xr_rows[1])
        load_scale_rows(nc, s2_raw, w2_scales, range(4))
        nc.sync.dma_start(out=w2_raw[:].bitcast(I32), in_=w2_words[0].bitcast(I32))
        nc.sync.dma_start(out=res[2][:], in_=xr_rows[2])
        nc.sync.dma_start(out=res[3][:], in_=xr_rows[3])
        nc.sync.dma_start(out=g2[:], in_=gate2)

        nc.vector.memset(zero[:], 0.0)
        zeros = zero[:].to_broadcast([P, T])
        for w in win1[:2]:
            nc.vector.memset(w[:], 0.0)
        for w in win1[2:] + win2:
            nc.scalar.activation(w[:], zeros, SILU)

        permute_columns(nc, w1[:].bitcast(U16), w1_raw[:].bitcast(U16))
        permute_columns(nc, s1[:], s1_raw[:])
        ident = tile([P, P], F32, "ident", "s1_raw")
        make_identity(nc, ident[:])

        nc.vector.tensor_copy(xw_g[:].bitcast(U32), xw[:].bitcast(U32).indirect(list1[:]))
        for slots in (A, BC):
            nc.vector.tensor_copy(xs_g[:, slots], xs[:].indirect(entries(list1, slots)))

        def product(n, words, scales, codes, code_scales, act, t, slots):
            acc = bank(n)
            for cols in (B, C) if slots == BC else (slots,):
                nc.tensor.matmul_mx(
                    out=acc[:, cols],
                    lhsT=words[:, 2 * P * t : 2 * P * (t + 1)].bitcast(FP4X4),
                    lhsT_scale=scales[:, P * t : P * (t + 1)],
                    rhs=codes[:, cols].bitcast(FP8X4),
                    rhs_scale=code_scales[:, cols],
                    start=True,
                    stop=True,
                )
            nc.scalar.activation(act[t][:, slots], acc[:, slots], SILU)

        def scatter(window, offsets, act, g, slots):
            nc.vector.tensor_tensor(window[:].indirect(entries(offsets, slots)), act[:, slots], g[:, slots], MULT)

        def turn(dst, src, start, stop):
            for j in range(BANK // P):
                cols = slice(P * j, P * (j + 1))
                nc.tensor.matmul(
                    dst[:, cols], src[:, cols], ident[:],
                    start=start and j == 0, stop=stop and j == BANK // P - 1, is_transpose=True,
                )

        def plane(t, slots):
            if slots == A:
                return grouped_a[:, :, t]
            return grouped_bc[:, slots.start - P : slots.stop - P, t]

        def gather_r(t, slots):
            nc.scalar.activation(plane(t, slots), r_bf[t][:].indirect(entries(list2, slots)), COPY)

        r_turned, r_bf = {}, {}

        def open_r(t):
            sums = [bank(2 + 2 * t + h) for h in range(2)]
            for h in range(2):
                turn(sums[h], res[t][:, HALVES[h]], True, False)
            return sums

        def close_r(t, sums):
            r_turned[t] = tile([P, T], F32, "r_turned%d" % t)
            r_bf[t] = tile([P, T], BF16, "r_bf%d" % t)
            for h in range(2):
                turn(sums[h], win1[t][:, HALVES[h]], False, True)
                nc.scalar.copy(r_turned[t][:, HALVES[h]], sums[h][:])
            for h in range(2):
                back = bank(6 + h)
                turn(back, r_turned[t][:, HALVES[h]], True, True)
                nc.scalar.copy(r_bf[t][:, HALVES[h]], back[:])

        pieces1 = [(0, A), (1, A), (0, BC), (1, BC), (2, WHOLE), (3, WHOLE)]
        for n, (t, slots) in enumerate(pieces1):
            product(n, w1, s1, xw_g, xs_g, y, t, slots)
        win2.append(tile([P, T], F32, "win2_2", "xs_g"))
        nc.scalar.activation(win2[2][:], zeros, SILU)
        sums0 = open_r(0)
        for t, slots in pieces1[:3]:
            scatter(win1[t], list1, y[t], g1, slots)
        close_r(0, sums0)
        gather_r(0, A)
        gather_r(0, BC)
        scatter(win1[1], list1, y[1], g1, BC)
        y_gated = tile([P, 2, S], F32, "y_gated", "win1_0")
        nc.vector.tensor_tensor(y_gated[:], y_late[:], g1[:].unsqueeze(1).to_broadcast([P, 2, S]), MULT)
        r_bf[1] = tile([P, T], BF16, "r_bf1", "y_late")
        nc.gpsimd.tensor_tensor(r_bf[1][:], res[1][:], win1[1][:], ADD)
        gather_r(1, A)
        gather_r(1, BC)
        r_turned[1] = tile([P, T], F32, "r_turned1")
        for h in range(2):
            sums = bank(3 - h)
            turn(sums, res[1][:, HALVES[h]], True, False)
            turn(sums, win1[1][:, HALVES[h]], False, True)
            nc.scalar.copy(r_turned[1][:, HALVES[h]], sums[:])
        nc.vector.tensor_copy(win1[2][:].indirect(list1[:]), y_gated[:, 0, :])
        r_bf[2] = tile([P, T], BF16, "r_bf2")
        nc.gpsimd.tensor_tensor(r_bf[2][:], res[2][:], win1[2][:], ADD)
        sums2 = [bank(6 + h) for h in range(2)]
        for h in range(2):
            turn(sums2[h], res[2][:, HALVES[h]], True, False)
        for h in range(2):
            turn(sums2[h], win1[2][:, HALVES[h]], False, False)
        nc.vector.tensor_copy(win1[1][:].indirect(list1[:]), y_gated[:, 1, :])
        r_bf[LAST] = tile([P, T], BF16, "r_bf3", "res2")
        nc.vector.tensor_tensor(r_bf[LAST][:], res[LAST][:], win1[1][:], ADD)
        w2 = tile([P, 2 * K], U8, "w2", "win1_2")
        permute_columns(nc, w2[:].bitcast(U16), w2_raw[:].bitcast(U16))
        s2 = tile([P, K], U8, "s2", "w2_raw")
        permute_columns(nc, s2[:], s2_raw[:])

        def quantize(cols):
            src = grouped_a[:] if cols == A else grouped_bc[:, cols.start - P : cols.stop - P, :]
            nc.vector.quantize_mx(
                out=r_codes[:, cols].bitcast(FP8X4),
                scales=r_scales[:, cols],
                in_=src.rearrange("p s t -> p (s t)"),
            )

        def second(n, t, slots):
            product(n, w2, s2, r_codes, r_scales, z, t, slots)

        gather_r(2, A)
        gather_r(3, A)
        quantize(A)
        r_last = tile([P, T], F32, "r_last", "grouped_a")
        nc.vector.tensor_tensor(r_last[:], res[LAST][:], win1[1][:], ADD)
        gather_r(2, B)
        gather_r(3, B)
        quantize(B)
        second(0, 2, A)
        second(1, 0, A)
        gather_r(2, C)
        second(0, 2, B)
        second(1, 0, B)
        gather_r(3, C)
        scatter(win2[0], list2, z[2], g2, A)
        scatter(win2[1], list2, z[0], g2, A)
        scatter(win2[0], list2, z[2], g2, B)
        quantize(C)
        second(2, 2, C)
        second(3, 0, C)
        second(4, 1, WHOLE)
        second(5, 3, WHOLE)

        def store(t, sums, h, o):
            nc.scalar.copy(o[:, HALVES[h]], sums[:])
            nc.sync.dma_start(out=out_rows[t][:, HALVES[h]], in_=o[:, HALVES[h]])

        def open_out(t):
            sums = [bank(2 + 2 * t + h) for h in range(2)]
            for h in range(2):
                turn(sums[h], r_turned[t][:, HALVES[h]], True, False)
            return sums

        def close_out(t, window, sums, banks):
            turned = tile([P, T], F32, "turned")
            o = tile([P, T], F32, "o%d" % t)
            for h in range(2):
                fwd = bank(banks[h])
                turn(fwd, window[:, HALVES[h]], True, True)
                nc.scalar.copy(turned[:, HALVES[h]], fwd[:])
            for h in range(2):
                turn(sums[h], turned[:, HALVES[h]], False, True)
                store(t, sums[h], h, o)

        def close_forward(t, window, sums, banks):
            turned = tile([P, T], F32, "turned")
            o = tile([P, T], F32, "o%d" % t)
            for h in range(2):
                turn(sums[h], window[:, HALVES[h]], False, True)
                nc.scalar.copy(turned[:, HALVES[h]], sums[h][:])
            for h in range(2):
                back = bank(banks[h])
                turn(back, turned[:, HALVES[h]], True, True)
                store(t, back, h, o)

        sums0 = open_out(0)
        sums1 = open_out(1)
        scatter(win2[1], list2, z[0], g2, B)
        scatter(win2[0], list2, z[2], g2, C)
        close_forward(2, win2[0], sums2, (0, 1))
        scatter(win2[1], list2, z[0], g2, C)
        close_out(0, win2[1], sums0, (7, 6))
        scatter(win2[2], list2, z[1], g2, WHOLE)
        close_out(1, win2[2], sums1, (6, 7))
        scatter(win2[0], list2, z[3], g2, WHOLE)
        o_last = tile([P, T], F32, "o_last", "turned")
        for cols in (slice(0, 512), slice(512, 768), slice(768, T)):
            nc.vector.tensor_tensor(o_last[:, cols], r_last[:, cols], win2[0][:, cols], ADD)
            nc.sync.dma_start(out=out_rows[LAST][:, cols], in_=o_last[:, cols])
